import numpy as np, ml_dtypes
CORES = [5,29,101,125,133,157,229,253]
N = 8
BF = ml_dtypes.bfloat16
def gentries(a):
    return np.ascontiguousarray(a.reshape(8, 16, -1).transpose(0, 2, 1)).reshape(8, -1)
def gtable(e):
    e = np.asarray(e); return np.ascontiguousarray(e.reshape(8, -1, 16).transpose(0, 2, 1)).reshape(128, -1).astype(np.int32)
V, K, C, M, T, H, LX = 2048, 4096, 32, 3, 5, 2, 255
TH = np.array([62, 66])
LA = K // C
def parts(rng):
    w = np.floor(256 * rng.random((N, 8, 16, V)) * rng.random((N, 8, 16, V)))
    l = 1 + np.floor(LX * rng.random((N, 8, V)) * rng.random((N, 8, V))).astype(np.int64)
    d = np.argsort(rng.random((N, 8, M, V)), axis=-1)
    o = np.floor(LX * rng.random((N, 8, M, V)) * rng.random((N, 8, M, V))).astype(np.int64)
    b = rng.integers(0, V, (N, 8, LA, C)); c = np.floor(LX * rng.random((N, 8, LA, C)) * rng.random((N, 8, LA, C))).astype(np.int64)
    return w, l, d, o, b, c
def pack(w, l, d, o, b, c):
    return {"wp": np.ascontiguousarray(w.reshape(N, 128, V)).astype(np.float32).astype(BF), "rl": np.ascontiguousarray(l).astype(np.int32),
            "dm": np.ascontiguousarray(d.reshape(N, 8, M * V)).astype(np.int32), "om": np.ascontiguousarray(o.reshape(N, 8, M * V)).astype(np.int32),
            "cb": np.stack([gtable(a.reshape(8, -1)) for a in b]), "co": np.stack([gtable(a.reshape(8, -1)) for a in c])}
def setup_inputs(rng):
    return pack(*parts(rng))
def setup_inputs_spread(rng):
    bits = LX.bit_length()
    w = np.floor(np.exp2(8 * rng.random((N, 8, 1, V))) * rng.random((N, 8, 16, V)) * (rng.random((N, 8, 1, V)) > 0.0625))
    l = np.floor(np.exp2(bits * rng.random((N, 8, V)))).astype(np.int64)
    d = np.floor(V * rng.random((N, 8, M, V)) ** 3).astype(np.int64)
    o = np.floor(np.exp2(bits * rng.random((N, 8, M, V)))).astype(np.int64) - 1
    b = V - 1 - np.floor(V * rng.random((N, 8, LA, C)) ** 3).astype(np.int64)
    c = np.floor(np.exp2(bits * rng.random((N, 8, LA, C)))).astype(np.int64) - 1
    return pack(w, np.clip(l, 1, LX), np.clip(d, 0, V - 1), np.clip(o, 0, LX - 1), np.clip(b, 0, V - 1), np.clip(c, 0, LX - 1))
def setup_inputs_ends(rng):
    def ends(lo, hi, *shape): return np.where(rng.random(shape) < 0.5, lo, hi)
    s0 = V // 4; n0 = V * 3 // 8; mid = slice(s0, s0 + n0)
    share = np.broadcast_to(np.where(rng.random((N, 1, 1, V)) < 0.5, 0.9, 0.1), (N, 8, 16, V)).copy(); share[:, :, [3, 8, 15]] = 0.005
    w = np.where(rng.random((N, 8, 16, V)) < share, 255, 0); w[..., 0] = 0; w[..., V - 1] = 0
    full = [V - 1 if q % 2 == 1 or q == N - 1 else 0 for q in range(N)]
    for q in range(N): w[q, :, :, full[q]] = 255
    l = ends(1, LX, N, 8, V); l[..., mid] = ends(1, LX, N, 1, n0)
    d = ends(0, V - 1, N, 8, M, V); d[..., mid] = s0 + rng.integers(0, n0 - H, (N, 1, M, n0))
    o = ends(0, LX - 1, N, 8, M, V); o[..., mid] = ends(0, LX - 1, N, 1, M, n0)
    b = ends(0, V - 1, N, 8, LA, C); c = ends(0, LX - 1, N, 8, LA, C)
    quiet = rng.permutation(np.arange(3, LA - 2))[:LA * 3 // 8]; nq = len(quiet)
    b[:, :, quiet] = s0 + rng.integers(0, n0 - H, (N, 1, nq, C)); c[:, :, quiet] = ends(0, LX - 1, N, 1, nq, C)
    for i in (0, 1, 2, LA - 2, LA - 1):
        for q in range(N): b[q, :, i] = np.where((np.arange(C) + i + (LA - 1) + (C - 1)) % 2 == 0, full[q], V - 1 - full[q])
    return pack(w, l, d, o, b, c)
def setup_inputs_brink(rng):
    w, l, d, o, b, c = parts(rng); n8 = V // 8
    levels = np.array(sorted(set([0, 1, 127, 128] + [int(v) for h in TH for v in (h - 1, h, 128 - h, 129 - h)])))
    lev = np.repeat(rng.choice(levels, (N, n8)), 8, axis=1)[:, None, None, :]
    late = np.zeros((N, 8, 16)); late[0::4, :, 8:] = 1; late[1::4, :, :8] = 1; late[2::4, 4:] = 1
    pos = np.argsort(np.argsort((rng.random((N, 8, 16)) + late).reshape(N, 128), axis=1), axis=1).reshape(N, 8, 16, 1)
    lo = rng.integers(0, 255, (N, 8, 16, 1)); hi = lo + 1 + np.floor((255 - lo) * rng.random((N, 8, 16, 1))).astype(np.int64)
    rich = np.repeat(rng.random((N, n8)) < 0.3, 8, axis=1)[:, None, None, :]
    w = np.where(rich, w, np.where(pos < lev, hi, lo))
    d = 8 * np.repeat(np.argsort(rng.random((N, 1, M, n8)), axis=-1), 8, axis=-1) + rng.integers(0, 8 - H, (N, 8, M, V))
    b = 8 * rng.integers(0, n8, (N, 1, LA, C)) + rng.integers(0, 8 - H, (N, 8, LA, C))
    for g in range(8):
        s = g // 2
        if g % 2 == 0: lv, ov, cv = [max(s, 1), s + 1, s + 2], [0, 0, 1, s], [s, s, s + 1]
        else: lv, ov, cv = [LX - 1, LX], [0, 1, 2, LX - 1], [LX - 3, LX - 2, LX - 1]
        l[:, g] = rng.choice(np.array(lv), (N, V)); o[:, g] = rng.choice(np.array(ov), (N, M, V)); c[:, g] = rng.choice(np.array(cv), (N, LA, C))
    return pack(w, l, d, o, b, c)
def setup_inputs_corners(rng):
    w, l, d, o, b, c = parts(rng); v = np.arange(V)
    for q in range(N):
        for g in range(8):
            kd = (g + q) % 4; kl = (g // 2 + q) % 4; ko = (g + 2 * q) % 3; z = rng.random((M, V)) < 0.25
            if kd == 0: d[q, g, 0] = v; d[q, g, 1:] = v[::-1]
            elif kd == 1: d[q, g] = np.where(z, V - 1 - rng.integers(0, 3, (M, V)), d[q, g])
            elif kd == 2: d[q, g] = np.where(z, (V - 1) * rng.integers(0, 2, (M, V)), d[q, g])
            else: d[q, g] = (v[None, :] + 1 + np.arange(M)[:, None]) % V
            if kl == 0: l[q, g] = 1
            elif kl == 1: l[q, g] = LX
            elif kl == 2: l[q, g] = rng.choice(np.array([1, 2, LX - 1, LX]), V)
            else: l[q, g, V - 3:] = 1; l[q, g, :2] = (1, LX)
            if ko == 0: o[q, g] = 0
            elif ko == 1: o[q, g] = LX - 1
            else: o[q, g] = rng.choice(np.array([0, 1, LX - 2, LX - 1]), (M, V))
    c = np.where(rng.random(c.shape) < 0.5, rng.choice(np.array([0, 1, LX - 2, LX - 1]), c.shape), c)
    b = np.where(rng.random(b.shape) < 0.25, rng.choice(np.array([0, V - 2, V - 1]), b.shape), b)
    b[:, :, 0, 0] = 0; b[:, :, LA - 1, C - 1] = V - 1
    s = 256 // C; p = np.arange(128).reshape(8, 16, 1)
    w[2] = s * (C - 1 - (v - p) % C) + rng.integers(0, s, (8, 16, V))
    for g in range(8):
        bl = np.concatenate([[0], 1 + rng.permutation(LA - 2), [LA - 1]]) % (V // C)
        b[2, g] = C * bl[:, None] + np.arange(C)
    for g in (1, 4, 7):
        w[:, g, rng.integers(0, 16)] = np.where(rng.random((N, V)) * 2 * C < 1, rng.integers(1, 4, (N, V)), 0)
    w[1] = rng.integers(0, 4, (8, 16, 1))
    return pack(w, l, d, o, b, c)
def setup_inputs_crowd(rng):
    w, l, d, o, b, c = parts(rng)
    x = np.argsort(rng.random((N, 8, V)), axis=-1)[..., :3]; wide_x = np.ascontiguousarray(np.broadcast_to(x[:, :, None, :], (N, 8, M, 3)))
    prof = np.zeros((N, 8, 16, 3)); prof[..., 0] = 255; prof[..., 2] = 255
    for q in range(N): prof[q, rng.integers(0, 8), rng.integers(0, 16), 2] = 0
    np.put_along_axis(w, np.ascontiguousarray(np.broadcast_to(x[:, :, None, :], (N, 8, 16, 3))), prof, 3)
    np.put_along_axis(l, x, LX, 2); np.put_along_axis(o, wide_x, rng.integers(0, 4, (N, 8, M, 3)), 3)
    to = np.argsort(rng.random((N, 1, M, 3)), axis=-1); nx = np.broadcast_to(np.roll(x, -1, axis=0)[:, :, None, :], (N, 8, M, 3))
    np.put_along_axis(d, wide_x, np.take_along_axis(nx, np.ascontiguousarray(np.broadcast_to(to, (N, 8, M, 3))), 3), 3)
    one = rng.integers(0, 3, (N, 1, LA, C)); k = np.arange(C)
    one[:, :, LA - 1] = np.where(k % 2 == 1, 0, 1); one[:, :, LA - 2] = np.where(k % 2 == 1, 2, 1)
    one = np.broadcast_to(one, (N, 8, LA, C)).copy(); m = np.zeros((N, 8, LA, C), bool); m[:, :, LA * 3 // 10:] = True
    for q in range(1, N, 2):
        m[q, :3] = True; m[q, 3] = False; one[q, :2] = 0
        one[q, 1, rng.integers(0, LA - 1), rng.integers(0, C)] = 1; one[q, 2] = rng.integers(0, 3, (LA, C))
        m[q, 3, LA - 1] = True; one[q, 2:4, LA - 1] = 0; one[q, 4:, LA - 1] = np.where(k % 2 == 1, 1, 0)
    b = np.where(m, np.take_along_axis(x, one.reshape(N, 8, -1), 2).reshape(N, 8, LA, C), b); c = np.where(m, rng.integers(0, 4, c.shape), c)
    return pack(w, l, d, o, b, c)
def check_inputs(d):
    bad = []
    for k, lo, hi in (("wp", 0, 255), ("rl", 1, LX), ("dm", 0, V - 1), ("om", 0, LX - 1), ("cb", 0, V - 1), ("co", 0, LX - 1)):
        a = np.asarray(d[k]).astype(np.float64)
        if not (np.min(a) >= lo and np.max(a) <= hi): bad.append("range of " + k)
        elif np.any(a != np.floor(a)): bad.append("whole numbers in " + k)
    return bad
def reference(wp, rl, dm, om, cb, co):
    w = wp.astype(np.float32).reshape(N, 8, 16, V); ln = rl.astype(np.int64); dd = dm.astype(np.int64); oo = om.astype(np.int64)
    b = np.stack([gentries(a) for a in cb]).astype(np.int64); o = np.stack([gentries(a) for a in co]).astype(np.int64)
    e = np.zeros((N, 8, 16, LA), np.float32)
    for t in range(T):
        q = (np.arange(N) + t) % N; nx = (q + 1) % N
        x = np.take_along_axis(w[q], b[:, :, None, :], 3).reshape(N, 8, 16, LA, C)
        e = np.maximum(e, np.max(x, axis=4))
        a = np.add.reduce((x > np.roll(x, -1, axis=4)).astype(np.int64).reshape(N, 128, LA, C), axis=1)
        m = np.add.reduce((a[..., None] >= TH).astype(np.int64), axis=3).reshape(N, 1, K)
        ix = m * V + b
        b = np.take_along_axis(dd[q], ix, 2); o = o + np.take_along_axis(oo[q], ix, 2)
        for h in range(H):
            lb = np.take_along_axis(ln[nx], b, 2); hop = o >= lb
            o = np.where(hop, o - lb, o); b = np.where(hop, (b + 1) % V, b)
        o = np.minimum(o, np.take_along_axis(ln[nx], b, 2) - 1)
    return {"yb": np.stack([gtable(a) for a in b]).astype(np.float32), "yo": np.stack([gtable(a) for a in o]).astype(np.float32), "ye": e.reshape(N, 128, LA).astype(BF)}

from concourse.bass import DstId, RemoteDMATransfer
from concourse.mybir import AluOpType, AxisListType, ActivationFunctionType

ALU = AluOpType
ACT = ActivationFunctionType

N, V, STEPS, NQ = 8, 2048, 5, 4
QW, QL = 1024, 64
MS = 2064
H16 = "float16"
R_M1, R_L2, R_L1, R_L0, R_OM, R_HI, R_LO = 0, 1, 2, 3, 4, 5, 6
F_T1, F_T2, F_T3, F_L0, F_L1, F_D, F_OM = 0, 1, 2, 3, 4, 5, 6
NF = 7

PAR = {"gam": 1.56, "fac": 1.25, "hop": 6.5, "hop1": 3.3, "dma": 2.2, "sem": 0.12, "fix": 0.03, "slack": 0.25, "issue": 0.6,
       "g2n": 2, "osep": False, "seed": 0, "jit": 0.0, "late": True, "ftn": 1024, "anyg": True, "rlhop": 3.0, "lowsc": 0.0,
       "beta": 2.0, "betat": 0.0, "vpen": 0.0, "split": True, "hopsfirst": True, "lowft": 0.0, "wq": "act"}
PAR.update({"osep": True, "late": True, "split": False, "wq": "sync", "ftn": 1024})
PLAN = {'vec': '3 13 1 7 -3 -1 12 -28 14 5 -1 25 -5 -8 -7 13 58 -65 10 -24 26 -17 1 17 -9 55 31 -88 4 55 -50 -3 81 -92 70 -62 -7 5 90 -24 -48 -1 2 13 -10 -2 -7 104 -105 16 -5 8 -6 4 -8 9 -3 91 2 -94 66 -103 35 70 -104 132 -80 -1 10 -5 2 5 98 -3 -25 23 -51 -28 83 18 -99 27 -25 1 1 5 1 -4 24 1 1 5 1 -26 22 50 -26 1 1 5 1 -4 24 1 1 5 1 -4 18 -3 31 -3 -29 54 3 -51 50 -48 26 -23 25 23 -21 -25 1 1 5 1 20 -24 25 1 19 -2 -12 1 39 -43 19 26 -23 25 -55 -28 60 1 1 5 -11 8 4 20 1 1 5 1 -12 8 9 9 -3 25 6 -29 6 -3 31 -29 3 23 23 -44 23 -22 1 24 -22 3 1 35 -15 19 -18 1 42 -37 -3 17 3 -16 15 3 21 2 3 -24 1 1 21 -16 1 -4 22 21 -19 1 12 9 -20 25 -20 1 -4 43 3 -40 14 31 -29 3 17 -15 1 1 19 -17 3 1 15 24 -21 20 -36 18 1 1 5 1 13 -17 19 1 1 21 -18 1 1 17 -12 14 -13 -4 20 -1 24 -21 23 -21 1 1 51 -46 -3 18 2 -11 -5 18 1 1 -18 45 26 -24 -26 1 27 -26 4 1 24 1 1 4 1 15 -49 23 -22 73 -23 29 -26 -23 54 -53 21 3 26 23 -21 2 -28 1 1 4 1 24 -27 28 -27 28 4 1 -3 1', 'act': '95 25 -23 51 3 -26 25 29 -3 -124 129 -3 -127 32 5 -9 25 29 27 1 -16 43 -15 28 6 28 -23 25 3 51 3 -75 29 45 3 -64 43 -15 43 1 -16 34 31 -37 8 28 3 -21 44 -16 21 23 -59 61 3 -21 -15 43 -15 34 2 3 23 5 -21 44 3 -19 18 29 -3 -31 16 17 29 -34 15 21 32 -3 5 -3 -20 49 -18 20 -40 43 -41 29 41 -39 41 -3 -21 32 -20 2 29 2 4', 'pe': '96 -3 28 -22 25 -23 48 3 -25 53 -25 22 -127 79 28 26 2 -79 28 -24 6 22 6 18 4 24 -18 22 6 8 3 25 3 -25 50 -22 -26 51 -23 48 3 -74 49 -21 -24 6 22 19 26 -39 41 -23 4 24 -18 22 6 8 3 25 -22 25 -23 26 2 -23 46 -42 39 -15 -18 39 -17 39 3 -23 -13 39 -21 23 -19 6 18 18 3 -17 6 14 25 -23 20 -15 21 -17 19 20 3 -36 18 21 -17 19 -13 36 -3 -15 21 -17 19 -13 36 3 -21 24 -20 48 -26 23 -39 45 2 -26 52 -3 -18 -22 -5 7 29 15 -13 -7 48 -3 -23 29 2 -26 31 -27 5 26 -24 29 2', 'pool': '6 -1 2 1 1 196 -93 28 28 28 -22 -28 56 -84 109 28 -22 28 22 6 22 6 3 22 28 -22 28 22 6 31 -9 6 25 6 22 6 22 6 22 9 -3 32 31 67 -36 31', 'sync': '0 1 1 10 1 1 57 -1 -55 54 3 4 -2 -1 2 11 -1 5 -10 1 10 491 -1 31 1 66 -35 -1 31'}
PLAN = {'vec': '3 29 -11 12 -16 1 9 -3 -20 19 -7 31 -25 -2 14 64 -56 1 1 1 -26 107 -89 -2 60 -66 94 -95 12 -4 118 -108 -8 -8 9 2 141 -151 94 -100 75 51 -125 102 -75 1 1 13 34 -43 -3 2 -1 73 -69 -1 3 -1 4 1 -19 16 92 -107 16 38 81 -100 3 -10 2 3 7 42 55 -28 29 -28 45 -99 28 -26 1 1 5 21 -24 25 1 -22 27 -3 4 46 -26 1 1 5 1 -4 24 1 1 5 1 -4 15 28 -25 28 5 -28 48 -51 54 -52 26 -23 25 52 -49 -26 1 1 5 21 -24 25 1 13 -11 -24 27 1 16 28 -31 48 -46 26 -23 25 3 -26 1 1 5 1 20 1 1 -26 28 15 28 -40 15 28 -42 19 -45 42 31 -29 26 -23 25 3 -26 44 -43 1 70 -68 3 21 1 18 -17 5 -27 28 39 -43 48 -31 3 -1 -41 44 23 20 -41 23 -22 1 24 -22 3 1 20 1 1 5 -3 15 28 -25 -14 19 28 -31 26 -24 3 23 23 -21 -23 1 25 -24 70 -68 24 1 1 17 -40 28 -27 24 43 -39 16 -3 31 -29 26 2 -25 43 -41 1 1 5 1 -4 24 1 1 5 1 -4 15 31 -23 -5 36 -34 29 -27 3 26 26 -24 -26 1 28 -27 4 75 -50 -24 25 1 20 -16 -33 34 51 -84 6 47 -3 29 25 -52 -22 25 26 -50 52 3 -29 1 1 4 1 24 1 1 4 1 -34 1 30 1', 'act': '92 28 -26 3 25 26 31 -3 -26 3 25 3 -129 -1 27 5 5 16 28 28 1 -44 71 -43 28 28 6 28 -26 3 25 3 23 -44 28 44 3 -26 25 3 -64 28 15 28 19 28 -26 3 25 3 -39 18 28 16 28 -26 3 25 3 -21 -15 43 19 -34 62 -26 3 25 3 -39 18 44 -16 44 -26 3 25 3 -64 28 15 29 -1 -15 34 31 -29 3 28 3 -42 18 50 -19 50 -29 3 -43 71 3 -43 2 17 31 -19 2 29 2 4', 'pe': '93 3 25 3 -25 2 26 2 20 3 25 3 -25 -105 133 -26 28 -79 28 -24 28 -22 28 18 4 24 -18 22 6 8 3 25 3 -25 2 26 25 -23 20 -43 28 -24 28 39 3 -25 -39 28 13 26 2 -23 28 -24 6 22 14 3 25 3 -25 -14 16 26 2 -23 28 15 -39 42 25 -39 17 25 -23 -41 28 39 -21 23 -19 24 -18 22 14 3 25 3 -25 -14 16 26 2 -23 46 -3 -15 -24 67 -39 42 -25 -39 28 13 26 2 -23 4 6 18 4 6 8 3 28 3 -28 2 29 2 -26 52 -3 -18 -27 76 -71 74 -72 29 15 -20 22 -15 44 2 -26 31 -27 5 2 29 -5 7', 'pool': '5 1 2 1 -2 198 -93 28 -22 50 -22 50 -22 28 25 28 -22 28 59 -37 28 -22 28 25 28 -22 28 22 28 9 -31 28 25 28 -22 28 59 -37 28 -22 28 32 31 31 31 5', 'sync': '0 1 1 10 1 1 56 1 -56 61 -2 -2 1 2 -6 11 1 5 -1 5 1 490 1 30 1 30 1 30 5'}
R_OWN = 9

SCRATCH = {
    "f0": ("sbuf", [128, 3 * V], "bfloat16"), "id0": ("sbuf", [128, 128], "bfloat16"), "rlo": ("dram", [128, 128], "bfloat16"),
    "dh": ("sbuf", [128, 2, 192], "bfloat16"), "dq": ("sbuf", [128, 2, 192], "bfloat16"), "sel0": ("sbuf", [128, 8 * F_OM], "bfloat16"),
    "ztmp": ("sbuf", [128, 8], "bfloat16"), "dl": ("sbuf", [128, 256], "uint16"), "ho": ("sbuf", [128, 256], H16),
    "hi": ("sbuf", [128, 256], H16), "oph": ("sbuf", [128, 128], H16),
    "wt": ("sbuf", [128, 2064], "bfloat16"), "lw": ("sbuf", [128, 2080], "bfloat16"), "ft": ("sbuf", [128, 3 * MS], "bfloat16"),
    "ww": ("sbuf", [128, 4096], "bfloat16"), "cm": ("sbuf", [128, 4096], "bfloat16"), "sc": ("sbuf", [128, 4096], "bfloat16"),
    "fg": ("sbuf", [128, 4096], "bfloat16"), "msk": ("sbuf", [128, QW], "bfloat16"),
    "rli": ("sbuf", [128, 128], "int32"), "rlb": ("sbuf", [128, 128], "bfloat16"), "rln": ("dram", [128, 128], "bfloat16"),
    "rlx": ("sbuf", [128, 128], "bfloat16"), "omd": ("dram", [8, 3 * V], "bfloat16"),
    "cbi": ("sbuf", [128, 256], "int32"), "coi": ("sbuf", [128, 256], "int32"), "xo0": ("sbuf", [128, 512], "bfloat16"),
    "yd": ("sbuf", [128, 2, 192], "int32"), "yf": ("sbuf", [128, 24, 16], "float32"), "yt": ("sbuf", [128, 384], "float32"),
    "ld": ("sbuf", [128, 384], "uint16"), "omi": ("sbuf", [128, 384], "int32"), "omb": ("sbuf", [128, 384], "bfloat16"),
    "hii": ("sbuf", [128, 128], "int32"), "hij": ("sbuf", [128, 128], "int32"), "hl": ("sbuf", [128, 256], "bfloat16"),
    "dpc": ("sbuf", [128, 128], "float32"), "e2": ("sbuf", [128, 64], "float32"),
    "idp": ("sbuf", [128, 128], "bfloat16"), "idn": ("sbuf", [128, 128], "bfloat16"), "idm": ("sbuf", [128, 128], "bfloat16"),
    "idh": ("sbuf", [128, 128], H16), "w8": ("sbuf", [128, 8], "bfloat16"), "cst": ("sbuf", [128, 4, 64], H16),
    "self": ("sbuf", [128, 8 * NF], "bfloat16"), "stmp": ("sbuf", [128, 8], "bfloat16"),
    "sela": ("sbuf", [128, 128], "bfloat16"), "selo": ("sbuf", [128, 64], "bfloat16"), "mib": ("sbuf", [128, 2], "float32"),
    "bl": ("sbuf", [128, STEPS * 256], "uint16"), "ot": ("sbuf", [128, STEPS * 256], "bfloat16"),
    "bo": ("sbuf", [128, 4 * 256], "uint16"), "oo": ("sbuf", [128, 4 * 256], "bfloat16"),
    "ein": ("sbuf", [128, STEPS * 128], "bfloat16"), "eo": ("sbuf", [128, STEPS * 128], "bfloat16"),
    "bn": ("sbuf", [128, 256], H16), "ix": ("sbuf", [128, 256], "uint16"),
    "xc": ("sbuf", [128, 33, 8], "bfloat16"), "xd": ("sbuf", [128, 33, 8], H16), "xh": ("sbuf", [128, 65, 8], H16),
    "xq": ("sbuf", [128, 33, 8], "bfloat16"),
    "yy": ("sbuf", [128, 256], "bfloat16"), "op": ("sbuf", [128, 128], "bfloat16"), "wr": ("sbuf", [128, 128], "float32"),
    "fo": ("sbuf", [128, 512], "float32"), "fi": ("sbuf", [128, 512], "float32"),
    "df0": ("psum", [128, 512], "float32"), "df1": ("psum", [128, 512], "float32"), "df2": ("psum", [128, 512], "float32"),
    "vi0": ("psum", [128, 512], "float32"), "vi1": ("psum", [128, 512], "float32"),
    "fb0": ("psum", [128, 512], "float32"), "fb1": ("psum", [128, 512], "float32"), "lb": ("psum", [128, 512], "float32"),
}
SEMAPHORES = (["sv", "sa", "sp", "sg", "sent", "l_rl", "d_rl", "d_cb", "d_co", "d_dm", "d_wp", "d_om", "d_od", "d_hl", "d_lw", "d_ft",
               "d_out", "d_oa", "a_rl", "d_f0", "d_ro", "d_lo"]
              + ["a_b%d" % i for i in range(16)] + ["a_o%d" % i for i in range(16)]
              + ["a_e%d" % i for i in range(STEPS)] + ["a_f%d" % i for i in range(NQ)])
ENG_SEM = {"vec": "sv", "act": "sa", "pe": "sp", "pool": "sg"}


def bits(engines):
    m = 0
    for e in engines:
        m |= 1 << e
    return m


def helpers_of(T, topo, rank):
    me, nx, pv = T.cores[rank], T.cores[(rank + 1) % N], T.cores[(rank - 1) % N]
    hs = [c for c in topo.cores_of(me) if T.rank_of(c) is None and topo.may_write(c, nx) and topo.may_write(c, pv)]
    return sorted(hs, key=lambda c: (topo.die(c) != topo.die(me), c))


def relay_engines(topo, src, dst, role):
    e = topo.engines(src, dst)
    if PAR["osep"]:
        return e
    return e[:len(e) // 2] if role == 0 else e[len(e) // 2:]


def build_ops(g, T, topo, rank):
    ops = []
    lastw, readers = {}, {}
    age = [0.0]
    me = T.cores[rank]
    hs = helpers_of(T, topo, rank)
    hb, ho, he = hs[0], hs[1], hs[2]
    home = T.cores[(rank - (STEPS - 1)) % N]
    P = PAR
    cyc = 0.83e-3 * P["fac"]
    vec, act, pe, sync = g.vector, g.scalar, g.tensor, g.sync

    def add(alts, reads=(), writes=(), banks=(), sem=None, val=0, lat=0.0, after=(), low=0.0):
        i = len(ops)
        deps = {}
        for r in reads:
            if r in lastw:
                deps[lastw[r]] = True
        for w in writes:
            if w in lastw:
                deps[lastw[w]] = True
            for j in readers.get(w, ()):
                deps[j] = True
        for b in banks:
            if b in lastw:
                deps[lastw[b]] = deps.get(lastw[b], False)
        for r in reads:
            readers.setdefault(r, []).append(i)
        for w in list(writes) + list(banks):
            lastw[w] = i
            readers[w] = []
        ops.append({"i": i, "alts": alts, "eng": None, "deps": deps, "sem": sem, "val": val, "lat": lat, "after": list(after), "low": low + age[0]})
        return i

    def V_(fn, n, reads, writes, banks=(), low=0.0):
        return add({"vec": (fn, P["fix"] + max(64, n) * cyc)}, reads, writes, banks, low=low)

    def A_(fn, n, reads, writes, banks=()):
        return add({"act": (fn, 2 * P["fix"] + max(64, n) * cyc)}, reads, writes, banks)

    def copy_(out, in_, scale, n, reads, writes, banks=()):
        return add({"vec": (lambda: vec.tensor_scalar(out, in_, scale, None, ALU.mult), P["fix"] + max(64, n) * cyc),
                    "act": (lambda: act.activation(out, in_, ACT.Copy, scale=scale), 2 * P["fix"] + max(64, n) * cyc)}, reads, writes, banks)

    def G_(fn, n, reads, writes):
        return add({"pool": (fn, 0.15 + 2 * n * cyc)}, reads, writes)

    def mm_cols(ap):
        n = 1
        for d in list(ap.shape)[1:]:
            n *= int(d)
        return n

    def M_(mms, reads, banks):
        def fn():
            r = None
            for o, l, rh, s, e in mms:
                r = pe.matmul(o, l, rh[0]() if isinstance(rh, list) else rh, s, e)
            return r
        n = sum(max(64, mm_cols(mm[0])) for mm in mms)
        return add({"pe": (fn, n * cyc / 2)}, reads, (), banks)

    def D_(q, out, in_, sem, reads, writes, lat=None, order=None):
        e = sync if q == "sync" else act
        return add({q: (lambda: e.dma_start(out, in_), 0.1)}, reads, writes, [order] if order else (), sem=sem, val=16,
                   lat=P["dma"] if lat is None else lat)

    def gather(eng, out, win, off, n, reads, writes):
        alts = {"vec": (lambda: vec.tensor_copy(out, win.indirect(off)), 0.05 + n * P["gam"] * cyc),
                "act": (lambda: act.activation(out, win.indirect(off), ACT.Copy), 0.065 + n * P["gam"] * cyc)}
        return add(alts if eng == "any" else {eng: alts[eng]}, reads, writes)

    sent = [0]

    def send(items, reads, local="sent"):
        def fn():
            tr = []
            for dst, dst_ap, src_ap, sem, mask in items:
                rid, pid = topo.addr(dst, me)
                tr.append(RemoteDMATransfer(dst_ids=[DstId(rid=rid, pnc=pid)], dma_engine_mask=mask, remote_sem=T.sem[sem],
                                            src=src_ap, dst=dst_ap))
            g.remote_dma_fused(tr, local_sem=T.sem[local])
            return None
        if local == "sent":
            for it in items:
                sent[0] += bin(it[4]).count("1")
        return add({"pool": (fn, P["issue"])}, reads, (), ["to%d" % it[0] for it in items], sem="", val=0)

    def arrive(sem, val, writes, sender, lat):
        return add({}, (), writes, sem=sem, val=val, lat=lat, after=[sender])

    far = len(topo.engines(hb, T.cores[(rank + 1) % N]))
    m_home = topo.mask(me, home)
    m_b, m_o = bits(relay_engines(topo, me, hb, 0)), bits(relay_engines(topo, me, ho, 1))

    D_("sync", T.rli[:], T.rl[:], "d_rl", (), ["rli"], order="sync")
    split = P["split"]
    D_(P["wq"], T.cbi[:], T.cb[:], "d_cb", (), ["cbi"], lat=2.6, order=P["wq"])
    D_(P["wq"], T.wt[:, 0:V], T.wp[:], "d_wp", (), ["wt"], lat=4.5, order=P["wq"])
    V_(lambda: vec.memset(T.lw[:], -1.0), 1040, (), ["lw"])
    V_(lambda: vec.tensor_copy(T.rlb[:], T.rli[:]), 128, ["rli"], ["rlb"])
    G_(lambda: g.iota(T.dpc[:], [[-1, 128]], 0, 1, allow_small_or_imprecise_dtypes=True), 128, (), ["dpc"])
    G_(lambda: g.iota(T.hii[:], [[8, 16], [0, 8]], 0, 128), 128, (), ["hii"])
    G_(lambda: g.iota(T.hl[:, 128:256], [[0, 16], [1, 8]], 0, 0, allow_small_or_imprecise_dtypes=True), 128, (), ["hl1"])
    G_(lambda: g.iota(T.e2[:], [[-16, 8], [-1, 8]], 0, 1, allow_small_or_imprecise_dtypes=True), 64, (), ["e2"])
    s = send([(hb, T.rlx[:], T.rlb[:], "a_rl", topo.mask(me, hb))], ["rlb"], "l_rl")
    arrive("a_rl", far, ["rln"], s, P["hop"] + P["rlhop"])
    arrive("l_rl", len(topo.engines(me, hb)), ["rlgone"], s, 3.8)
    gone = ["rlgone"] if P["late"] else []
    more = 0.0 if P["late"] else 2.5
    for g1 in range(2):
        D_("sync", T.yd[:, g1, :], T.dm[g1::2, :], "d_dm", gone, ["yd%d" % g1], lat=3.0 + more, order="sync")
    D_("sync", T.omi[:], T.om[:], "d_om", gone, ["omi"], lat=4.2 + more, order="sync")
    D_("sync", T.coi[:], T.co[:], "d_co", ["rlgone"], ["coi"], lat=5.5, order="sync")
    for name, c in (("idp", 1.0), ("idn", -1.0), ("idh", 1.0), ("idm", float(MS))):
        V_(lambda name=name, c=c: vec.tensor_scalar(T[name][:], T.dpc[:], 0.0, c, ALU.is_equal, ALU.mult), 128, ["dpc"], [name])
    V_(lambda: vec.memset(T.w8[:], 0.125), 8, (), ["w8"])
    for v, c in ((0, 129.125), (1, 113.125)):
        V_(lambda v=v, c=c: vec.tensor_scalar(T.cst[0:64, 2 * v:2 * v + 2, :], T.dpc[0:64, :], 0.0, c, ALU.mult, ALU.add), 128, ["dpc"], ["cst%d" % v])
        V_(lambda v=v, c=c: vec.tensor_scalar(T.cst[64:128, v::2, :], T.dpc[64:128, :], 0.0, c, ALU.mult, ALU.add), 128, ["dpc"], ["cst%d" % (2 + v)])
    V_(lambda: vec.memset(T.msk[:], 1.0), 512, (), ["msk"])
    V_(lambda: vec.memset(T.msk[:, 0::32], 0.0), 32, (), ["msk"])
    V_(lambda: vec.memset(T.xc[:], 0.0), 132, (), ["xc0", "xc1"])
    V_(lambda: vec.memset(T.xq[:], 0.0), 132, (), ["xq0", "xq1"])
    V_(lambda: vec.tensor_copy(T.xd[:], T.xc[:]), 132, ["xc0", "xc1"], ["xd0", "xd1"])
    V_(lambda: vec.tensor_copy(T.xh[:, 0:33, :], T.xq[:]), 132, ["xq0", "xq1"], ["xh0a", "xh0b", "xh1a"])
    V_(lambda: vec.tensor_copy(T.xh[:, 32:65, :], T.xq[:]), 132, ["xq0", "xq1"], ["xh1a", "xh1b"])
    V_(lambda: vec.tensor_scalar(T.hij[:], T.hii[:], V - 1, None, ALU.bitwise_and), 128, ["hii"], ["hij"])
    V_(lambda: vec.tensor_copy(T.hl[:, 0:128], T.hij[:]), 128, ["hij"], ["hl0"])

    def I(f):
        return T.idp[:, f::16]

    def S(f):
        return T["self"][:, 8 * f:8 * f + 8]
    V_(lambda: vec.tensor_tensor(S(F_T1), I(R_L0), I(R_OM), ALU.add), 16, ["idp"], ["s0"])
    V_(lambda: vec.tensor_tensor(T.stmp[:], I(R_M1), I(R_L2), ALU.add), 16, ["idp"], ["stmp"])
    V_(lambda: vec.tensor_tensor(S(F_D), I(R_HI), I(R_LO), ALU.add), 16, ["idp"], ["s5"])
    V_(lambda: vec.tensor_tensor(S(F_T2), S(F_T1), I(R_L1), ALU.add), 16, ["idp", "s0"], ["s1"])
    V_(lambda: vec.tensor_copy(S(F_L0), I(R_L0)), 8, ["idp"], ["s3"])
    V_(lambda: vec.tensor_copy(S(F_L1), I(R_L1)), 8, ["idp"], ["s4"])
    V_(lambda: vec.tensor_copy(S(F_OM), I(R_OM)), 8, ["idp"], ["s6"])
    V_(lambda: vec.tensor_tensor(S(F_T3), S(F_T2), T.stmp[:], ALU.add), 16, ["s1", "stmp"], ["s2"])
    SEL = ["s%d" % f for f in range(NF)]
    for ib in range(2):
        V_(lambda ib=ib: vec.tensor_scalar(T.sela[:, 64 * ib:64 * ib + 64], T.e2[:], 8.0 * ib, None, ALU.is_equal), 64, ["e2"], ["sela%d" % ib])
    for ib in range(2):
        V_(lambda ib=ib: vec.tensor_reduce(T.mib[:, ib:ib + 1], T.sela[:, 64 * ib:64 * ib + 64], AxisListType.X, ALU.add), 64, ["sela%d" % ib], ["mib%d" % ib])
    V_(lambda: vec.tensor_tensor(T.selo[:], T.sela[:, 0:64], T.sela[:, 64:128], ALU.add), 128, ["sela0", "sela1"], ["selo"])
    V_(lambda: vec.tensor_copy(T.bl[:, 0:256], T.cbi[:]), 256, ["cbi"], ["bl0_%d" % k for k in range(NQ)])
    for ib in range(2):
        V_(lambda ib=ib: vec.tensor_scalar(T.xo0[:, ib::2], T.coi[:], T.mib[:, ib:ib + 1], None, ALU.mult), 256, ["coi", "mib%d" % ib], ["xo0%d" % ib])
    M_([(T.lb[:, 64 * k:64 * k + 64], T.xo0[:, 128 * k:128 * k + 128], T.selo[:], True, True) for k in range(NQ)], ["xo00", "xo01", "selo"], ["lb"])
    copy_(T.ot[:, 0:256], T.lb[:, 0:256], 1.0, 256, (), ["ot0_%d" % k for k in range(NQ)], ["lb"])
    copy_(T.wt[:, V:V + 16], T.wt[:, 0:16], 1.0, 16, ["wt"], ["wtx"])
    for g1 in range(2):
        V_(lambda g1=g1: vec.tensor_copy(T.yf[:, g1::2, :], T.yd[:, g1, :]), 192, ["yd%d" % g1], ["yf%d" % g1])
    V_(lambda: vec.transpose(T.yt[:], T.yf[:]), 384, ["yf0", "yf1"], ["yt"])
    for u in range(12):
        V_(lambda u=u: vec.tensor_copy(T.ld[:, u::12], T.yt[:, 32 * u:32 * u + 32]), 32, ["yt"], ["ld%d" % u])
    LD = ["ld%d" % u for u in range(12)]
    V_(lambda: vec.tensor_scalar(T.omb[:], T.omi[:], -1.0, None, ALU.mult), 384, ["omi"], ["omb"])
    D_("sync", T.omd[:], T.omb[:], "d_od", ["omb"], ["omd"])
    fill = ["f0a", "f0b", "f0c"]
    if split:
        V_(lambda: vec.memset(T.f0[:, 0:V], 0.0), 1024, (), ["f0a"])
        for j in (1, 2):
            A_(lambda j=j: act.activation(T.f0[:, V * j:V * j + V], T.lw[:, 0:V], ACT.Copy), V, ["lw"], [fill[j]])
    D_("sync", T.lw[R_HI::16, 16:16 + V], T.hl[:, 0:128], "d_hl", ["hl0", "lw", "rlgone"] + fill, ["lw5"])
    D_("sync", T.lw[R_LO::16, 16:16 + V], T.hl[:, 128:256], "d_hl", ["hl1", "lw", "rlgone"] + fill, ["lw6"])
    for h in range(3):
        D_("sync", T.lw[R_L0 - h::16, 16 - h:16 - h + V], T.rln[:], "d_lw", ["rln", "lw"] + fill, ["lwm%d" % h])
    for h in (1, 2):
        D_("sync", T.lw[R_L0 - h::16, 16 + V - h:18 + V - h], T.rln[0::16, 0:2], "d_lw", ["rln", "lw"] + fill, ["lwx%d" % h])
    LW = ["lw", "lw5", "lw6", "lwm0", "lwm1", "lwm2", "lwx1", "lwx2"]
    LO = ["lom0", "lom1", "lom2", "lox1", "lox2"]
    if split:
        D_("sync", T.rlo[:], T.rlb[:], "d_ro", ["rlb", "rlgone"], ["rlo"])
        for h in range(3):
            D_("sync", T.lw[R_OWN - h::16, 16 - h:16 - h + V], T.rlo[:], "d_lo", ["rlo", "lw"] + fill, ["lom%d" % h])
        for h in (1, 2):
            D_("sync", T.lw[R_OWN - h::16, 16 + V - h:18 + V - h], T.rlo[0::16, 0:2], "d_lo", ["rlo", "lw"] + fill, ["lox%d" % h])
        LW = LW + LO
    win_l = T.lw[:, 16:16 + V]
    FT = []
    nf = P["ftn"]
    age[0] = P["lowft"]
    for m in range(3):
        gather("vec", T.ft[:, MS * m + V:MS * m + MS], win_l, T.ld[:, 128 * m:128 * m + 1], 16, LW + LD, ["ftx%d" % m])
        parts = ["ft%d_%d" % (m, j) for j in range(V // nf)]
        for j in range(V // nf):
            gather("any" if P["anyg"] else ("vec", "act")[j % 2], T.ft[:, MS * m + nf * j:MS * m + nf * j + nf], win_l,
                   T.ld[:, 128 * m + nf // 16 * j:128 * m + nf // 16 * (j + 1)], nf, LW + LD, [parts[j]])
        D_("sync", T.ft[R_OM::16, MS * m + V:MS * m + MS], T.omd[:, V * m:V * m + 16], "d_ft", ["omd"], ["ftx%d" % m])
        D_("sync", T.ft[R_OM::16, MS * m:MS * m + V], T.omd[:, V * m:V * m + V], "d_ft", ["omd"], parts)
        FT += parts + ["ftx%d" % m]
    age[0] = 0.0
    F0, SEL0 = ["f0h0", "f0h1", "f0l0", "f0l1", "f0o"], ["z%d" % f for f in range(F_OM)]
    if split:
        V_(lambda: vec.tensor_scalar(T.id0[:], T.dpc[:], 0.0, float(V), ALU.is_equal, ALU.mult), 128, ["dpc"], ["id0"])
        V_(lambda: vec.tensor_copy(T.dh[:], T.yd[:]), 384, ["yd0", "yd1"], ["dh"])
        V_(lambda: vec.tensor_tensor(T.dq[:], T.yd[:], T.dh[:], ALU.subtract), 768, ["yd0", "yd1", "dh"], ["dq"])
        for g1 in range(2):
            D_("sync", T.f0[16 * g1 + R_HI::32, :], T.dh[:, g1, :], "d_f0", fill + ["dh"], ["f0h%d" % g1], lat=2.6)
            D_("sync", T.f0[16 * g1 + R_LO::32, :], T.dq[:, g1, :], "d_f0", fill + ["dq"], ["f0l%d" % g1], lat=3.0)
        D_("sync", T.f0[R_OM::16, :], T.omb[:], "d_f0", fill + ["omb"], ["f0o"], lat=3.0)

        def Z(f):
            return T.sel0[:, 8 * f:8 * f + 8]
        for f, row in ((F_T1, R_OWN), (F_L0, R_OWN), (F_L1, R_OWN - 1)):
            V_(lambda f=f, row=row: vec.tensor_copy(Z(f), I(row)), 8, ["idp"], ["z%d" % f])
        V_(lambda: vec.tensor_copy(Z(F_D), S(F_D)), 8, ["s5"], ["z5"])
        V_(lambda: vec.tensor_tensor(Z(F_T2), I(R_OWN), I(R_OWN - 1), ALU.add), 16, ["idp"], ["z1"])
        V_(lambda: vec.tensor_tensor(T.ztmp[:], I(R_M1), I(R_OWN - 2), ALU.add), 16, ["idp"], ["ztmp"])
        V_(lambda: vec.tensor_tensor(Z(F_T3), Z(F_T2), T.ztmp[:], ALU.add), 16, ["z1", "ztmp"], ["z2"])

    npiece = [0]
    pend = [None]

    def send_b(t, k, dst, name):
        n, c0 = NQ * t + k, 256 * t + QL * k
        items = [(hb, dst, T.bo[:, c0:c0 + QL], "a_b%d" % n, m_b)]
        rd = ["bo%d_%d" % (t, k)]
        if pend[0] is not None:
            items.append(pend[0][0])
            rd.append(pend[0][1])
        s = send(items, rd)
        arrive("a_b%d" % n, far, [name], s, P["hop"])
        if pend[0] is not None:
            arrive(pend[0][0][3], far, [pend[0][2]], s, P["hop"])
            pend[0] = None

    def send_o(t, k, dst, src, src_name, name):
        pend[0] = ((ho, dst, src, "a_o%d" % (NQ * t + k), m_o), src_name, name)
        if P["osep"] or k == NQ - 1:
            s = send([pend[0][0]], [src_name])
            arrive(pend[0][0][3], far, [name], s, P["hop"] + (1.5 if t + k == 0 else 0.0))
            pend[0] = None

    def fields(k, win, lst, c, reads):
        fgs = ["fg%d_%d" % (k, h) for h in range(P["g2n"])]
        nw, nl = QW // P["g2n"], QL // P["g2n"]
        for h in range(P["g2n"]):
            gather("any" if P["anyg"] else ("act", "vec")[h], T.fg[:, QW * k + nw * h:QW * k + nw * h + nw], win,
                   lst[:, c + nl * h:c + nl * h + nl], nw, reads, [fgs[h]])
        return fgs

    def hops(k, sel, reads, o_in, ot):
        w0, sl = QW * k, k % 2
        fb = "fb%d" % sl
        M_([(T[fb][:, r:64 * F_OM:8], T.fg[:, w0 + r:w0 + QW:8], sel, True, True) for r in range(8)], reads, [fb])

        def FB(f, n=1):
            return T[fb][:, 64 * f:64 * (f + n)]
        x0 = 32 * sl
        h1, h2 = T.xh[:, x0 + 1:x0 + 16:2, :], T.xh[:, x0 + 17:x0 + 32:2, :]
        ha, hb_ = "xh%da" % sl, "xh%db" % sl
        V_(lambda: vec.tensor_tensor(h1, o_in, FB(F_T1), ALU.is_ge), 64, [ot], [ha], [fb])
        V_(lambda: vec.tensor_tensor(h2, o_in, FB(F_T2), ALU.is_ge), 64, [ot], [hb_], [fb])
        V_(lambda: vec.tensor_tensor(T.xd[:, 16 * sl + 1:16 * sl + 16:2, :], h1, FB(F_D), ALU.add), 64, [ha], ["xd%d" % sl], [fb])
        M_([(T.lb[:, 0:64], T.xh[:, x0 + 17:x0 + 33, :], T.idh[:, 0::2], True, False),
            (T.lb[:, 0:64], T.xh[:, x0 + 16:x0 + 32, :], T.idh[:, 1::2], False, False),
            (T.lb[:, 0:64], T.xd[:, 16 * sl + 1:16 * sl + 17, :], T.idh[:, 0::2], False, False),
            (T.lb[:, 0:64], T.xd[:, 16 * sl:16 * sl + 16, :], T.idh[:, 1::2], False, True)], ["idh", hb_, "xd%d" % sl], ["lb"])
        return FB, x0, ha, hb_

    def late_hops(k):
        c0, sl = QL * k, k % 2
        fb = "fb%d" % sl
        fgs = fields(k, win_l, T.dl, c0, LW + LO + ["dl%d" % k])
        o_in = T.hi[:, c0:c0 + QL]
        FB, x0, ha, hb_ = hops(k, T.sel0[:], SEL0 + fgs, o_in, "hi%d" % k)
        V_(lambda: vec.tensor_copy(T.bl[:, 256 + c0:256 + c0 + QL], T.lb[:, 0:64]), 64, (), ["bl1_%d" % k], ["lb"])
        V_(lambda: vec.tensor_tensor(T.oph[:, 64 * sl:64 * sl + 64], o_in, FB(F_T3), ALU.min), 64, ["hi%d" % k], ["oph%d" % sl], [fb])
        V_(lambda: vec.tensor_tensor(T.yy[:, 128 * sl:128 * sl + 128], T.xh[:, x0 + 1:x0 + 32:2, :], FB(F_L0, 2), ALU.mult), 128,
           [ha, hb_], ["yy%d" % sl], [fb])
        M_([(FB(F_OM), T.idh[:], T.oph[:, 64 * sl:64 * sl + 64], True, False),
            (FB(F_OM), T.idn[:], T.yy[:, 128 * sl:128 * sl + 64], False, False),
            (FB(F_OM), T.idn[:], T.yy[:, 128 * sl + 64:128 * sl + 128], False, True)], ["idh", "idn", "oph%d" % sl, "yy%d" % sl], [fb])
        copy_(T.ot[:, 256 + c0:256 + c0 + QL], FB(F_OM), 1.0, 64, (), ["ot1_%d" % k], [fb])

    for t in range(STEPS):
        last = t == STEPS - 1
        early = split and t == 0
        ms, idm = (V, "id0") if early else (MS, "idm")
        if split and t == 1 and P["hopsfirst"]:
            for k in range(NQ):
                age[0] = P["beta"] * k + P["betat"] * t
                late_hops(k)
        for k in range(NQ):
            c0, w0, sl = 256 * t + QL * k, QW * k, k % 2
            age[0] = P["beta"] * k + P["betat"] * t
            if split and t == 1 and not P["hopsfirst"]:
                late_hops(k)
            bl, ot = "bl%d_%d" % (t, k), "ot%d_%d" % (t, k)
            win_w = T.wt[:, 0:V] if t == 0 else T.wt[:, 0:V + 16]
            wr_ = ["wt"] if t == 0 else ["wt", "wtx"]
            vi, fb = "vi%d" % sl, "fb%d" % sl
            cmo = []
            for h in range(2):
                a = w0 + 512 * h
                gather("any" if P["anyg"] else ("vec", "act")[h], T.ww[:, a:a + 512], win_w, T.bl[:, c0 + 32 * h:c0 + 32 * h + 32], 512,
                       wr_ + [bl], ["ww%d_%d" % (k, h)])
                df = "df%d" % (npiece[0] % 3)
                npiece[0] += 1
                M_([(T[df][:, 0:512], T.idp[:], T.ww[:, a:a + 512], True, False),
                    (T[df][:, 0:511], T.idn[:], T.ww[:, a + 1:a + 512], False, False),
                    (T[df][:, 31:511:32], T.idp[:], T.ww[:, a + 32:a + 512:32], False, False),
                    (T[df][:, 31:512:32], T.idn[:], T.ww[:, a:a + 512:32], False, True)], ["idp", "idn", "ww%d_%d" % (k, h)], [df])
                cmo.append(add({"act": (lambda a=a, df=df: act.activation(T.cm[:, a:a + 512], T[df][:], ACT.Sign, bias=-0.5), 2 * P["fix"] + 512 * cyc),
                                "vec": (lambda a=a, df=df: vec.tensor_scalar(T.cm[:, a:a + 512], T[df][:], 0.0, 2.0, ALU.is_gt, ALU.mult),
                                        P["fix"] + 512 * cyc)}, (), ["cm%d_%d" % (k, h)], [df]))
            src_b = T.cbi[:, QL * k:QL * k + QL] if t == 0 else T.bl[:, c0:c0 + QL]
            V_(lambda k=k, src_b=src_b: vec.tensor_scalar(T.bn[:, QL * k:QL * k + QL], src_b, -1024.0, None, ALU.add), 64,
               ["cbi" if t == 0 else bl], ["bn%d" % k])
            M_([(T[vi][:, 0:64], T.idh[:], [lambda cmo=cmo: T.cst[:, 2 * (ops[cmo[0]]["eng"] == "vec") + (ops[cmo[1]]["eng"] == "vec"), :]], True, False)]
               + [(T[vi][:, r:64:8], T.cm[:, w0 + r:w0 + QW:8], T.w8[:], False, r == 7) for r in range(8)],
               ["idh", "cst0", "cst1", "cst2", "cst3", "w8", "cm%d_0" % k, "cm%d_1" % k], [vi])
            V_(lambda vi=vi, sl=sl: vec.tensor_scalar(T.xc[:, 16 * sl + 1:16 * sl + 16:2, :], T[vi][:, 0:64], 128.0, 130.0, ALU.max, ALU.min), 64,
               (), ["xc%d" % sl], [vi])
            M_([(T[vi][:, 64:128], T.idh[:], T.bn[:, QL * k:QL * k + QL], True, False),
                (T[vi][:, 64:128], T.xc[:, 16 * sl + 1:16 * sl + 17, :], T[idm][:, 0::2], False, False),
                (T[vi][:, 64:128], T.xc[:, 16 * sl:16 * sl + 16, :], T[idm][:, 1::2], False, True)],
               ["idh", idm, "bn%d" % k, "xc%d" % sl], [vi])
            V_(lambda vi=vi, k=k, ms=ms: vec.tensor_scalar(T.ix[:, QL * k:QL * k + QL], T[vi][:, 64:128], 1024.0 - 128.0 * ms, None, ALU.add), 64,
               (), ["ix%d" % k], [vi])
            V_(lambda w0=w0: vec.tensor_tensor_scan(T.sc[:, w0:w0 + QW], T.msk[:], T.ww[:, w0:w0 + QW], 0.0, ALU.mult, ALU.max), 512,
               ["msk", "ww%d_0" % k, "ww%d_1" % k], ["sc%d" % k], low=P["lowsc"])
            if early:
                fgs = fields(k, T.f0[:], T.ix, QL * k, F0 + ["ix%d" % k])
                M_([(T[fb][:, r:128:8], T.fg[:, w0 + r:w0 + QW:8], T["self"][:, 8 * F_D:8 * NF], True, True) for r in range(8)], SEL + fgs, [fb])
                V_(lambda sl=sl, fb=fb: vec.tensor_copy(T.xd[:, 16 * sl + 1:16 * sl + 16:2, :], T[fb][:, 0:64]), 64, (), ["xd%d" % sl], [fb])
                M_([(T.lb[:, 0:64], T.xd[:, 16 * sl + 1:16 * sl + 17, :], T.idh[:, 0::2], True, False),
                    (T.lb[:, 0:64], T.xd[:, 16 * sl:16 * sl + 16, :], T.idh[:, 1::2], False, True)], ["idh", "xd%d" % sl], ["lb"])
                V_(lambda c0=c0: vec.tensor_copy(T.bo[:, c0:c0 + QL], T.lb[:, 0:64]), 64, (), ["bo0_%d" % k], ["lb"])
                send_b(0, k, T.dl[:, c0:c0 + QL], "dl%d" % k)
                V_(lambda c0=c0, fb=fb: vec.tensor_tensor(T.ho[:, c0:c0 + QL], T.ot[:, c0:c0 + QL], T[fb][:, 64:128], ALU.subtract), 64,
                   [ot], ["ho%d" % k], [fb])
                send_o(0, k, T.hi[:, c0:c0 + QL], T.ho[:, c0:c0 + QL], "ho%d" % k, "hi%d" % k)
                continue
            fgs = fields(k, T.ft[:, 0:3 * MS], T.ix, QL * k, FT + ["ix%d" % k])
            o_in = T.ot[:, c0:c0 + QL]
            FB, x0, ha, hb_ = hops(k, T["self"][:, 0:8 * F_OM], SEL + fgs, o_in, ot)
            if not last:
                V_(lambda c0=c0: vec.tensor_copy(T.bo[:, c0:c0 + QL], T.lb[:, 0:64]), 64, (), ["bo%d_%d" % (t, k)], ["lb"])
                send_b(t, k, T.bl[:, 256 + c0:256 + c0 + QL], "bl%d_%d" % (t + 1, k))
            else:
                V_(lambda sl=sl: vec.tensor_scalar(T.wr[:, 64 * sl:64 * sl + 64], T.lb[:, 0:64], float(V), -float(V), ALU.is_ge, ALU.mult), 64,
                   (), ["wr%d" % sl], ["lb"])
                V_(lambda sl=sl, k=k: vec.tensor_tensor(T.fo[:, 128 * k:128 * k + 64], T.wr[:, 64 * sl:64 * sl + 64], T.lb[:, 0:64], ALU.add), 64,
                   ["wr%d" % sl], ["fob%d" % k], ["lb"])
            V_(lambda sl=sl, o_in=o_in, FB=FB: vec.tensor_tensor(T.op[:, 64 * sl:64 * sl + 64], o_in, FB(F_T3), ALU.min), 64, [ot], ["op%d" % sl], [fb])
            V_(lambda sl=sl, x0=x0, FB=FB: vec.tensor_tensor(T.yy[:, 128 * sl:128 * sl + 128], T.xh[:, x0 + 1:x0 + 32:2, :], FB(F_L0, 2), ALU.mult), 128,
               [ha, hb_], ["yy%d" % sl], [fb])
            M_([(FB(F_OM), T.idn[:], T.op[:, 64 * sl:64 * sl + 64], True, False)]
               + [(T[fb][:, 64 * F_OM + r:64 * NF:8], T.fg[:, w0 + r:w0 + QW:8], S(F_OM), False, False) for r in range(8)]
               + [(FB(F_OM), T.idp[:], T.yy[:, 128 * sl:128 * sl + 64], False, False),
                  (FB(F_OM), T.idp[:], T.yy[:, 128 * sl + 64:128 * sl + 128], False, True)],
               ["idp", "idn", "s6", "op%d" % sl, "yy%d" % sl] + fgs, [fb])
            if not last:
                copy_(T.oo[:, c0:c0 + QL], FB(F_OM), -1.0, 64, (), ["oo%d_%d" % (t, k)], [fb])
                send_o(t, k, T.ot[:, 256 + c0:256 + c0 + QL], T.oo[:, c0:c0 + QL], "oo%d_%d" % (t, k), "ot%d_%d" % (t + 1, k))
            else:
                copy_(T.xq[:, 16 * sl + 1:16 * sl + 16:2, :], FB(F_OM), -1.0, 64, (), ["xq%d" % sl], [fb])
                M_([(T[vi][:, 128:192], T.xq[:, 16 * sl + 1:16 * sl + 17, :], T.idp[:, 0::2], True, False),
                    (T[vi][:, 128:192], T.xq[:, 16 * sl:16 * sl + 16, :], T.idp[:, 1::2], False, True)], ["idp", "xq%d" % sl], [vi])
                copy_(T.fo[:, 128 * k + 64:128 * k + 128], T[vi][:, 128:192], 1.0, 64, (), ["foo%d" % k], [vi])
                s = send([(home, T.fi[:, 128 * k:128 * k + 128], T.fo[:, 128 * k:128 * k + 128], "a_f%d" % k, m_home)], ["fob%d" % k, "foo%d" % k])
                arrive("a_f%d" % k, far, ["fi%d" % k], s, P["hop1"])
                D_("sync", T.yb[:, QL * k:QL * k + QL], T.fi[:, 128 * k:128 * k + 64], "d_out", ["fi%d" % k], ())
                D_("act" if k == NQ - 1 else "sync", T.yo[:, QL * k:QL * k + QL], T.fi[:, 128 * k + 64:128 * k + 128],
                   "d_oa" if k == NQ - 1 else "d_out", ["fi%d" % k], ())
        e0 = 128 * t
        scs = ["sc%d" % k for k in range(NQ)]
        if t == 0:
            V_(lambda: vec.tensor_copy(T.eo[:, 0:128], T.sc[:, 31::32]), 64, scs, ["eo0"])
        else:
            V_(lambda e0=e0: vec.tensor_tensor(T.eo[:, e0:e0 + 128], T.sc[:, 31::32], T.ein[:, e0 - 128:e0], ALU.max), 256,
               scs + ["ein%d" % (t - 1)], ["eo%d" % t])
        dst = home if last else he
        s = send([(dst, T.ein[:, e0:e0 + 128], T.eo[:, e0:e0 + 128], "a_e%d" % t, topo.mask(me, dst))], ["eo%d" % t])
        arrive("a_e%d" % t, far, ["ein%d" % t], s, P["hop1"] if last else P["hop"])
    D_("sync", T.ye[:], T.ein[:, 128 * (STEPS - 1):128 * STEPS], "d_out", ["ein%d" % (STEPS - 1)], ())
    return ops, sent[0]


def schedule(ops):
    P = PAR
    groups = {}
    for o in ops:
        if o["alts"] and o["val"]:
            groups.setdefault(o["sem"], []).append(o["i"])
    if PLAN:
        order = {}
        for e, text in PLAN.items():
            order[e], i = [], 0
            for d in text.split():
                i += int(d)
                order[e].append(i)
                ops[i]["eng"] = e
        return order, groups
    pre = []
    for o in ops:
        d = set(o["deps"]) | set(o["after"])
        for j in list(d):
            if ops[j]["alts"] and ops[j]["val"] and ops[j]["sem"] != o["sem"] and o["deps"].get(j, False):
                d |= set(groups[ops[j]["sem"]])
        pre.append(d)
    suc = [[] for _ in ops]
    for o in ops:
        for j in pre[o["i"]]:
            suc[j].append(o["i"])
    left = [len(p) for p in pre]
    seq, stack, cnt = [], [i for i, n in enumerate(left) if n == 0], list(left)
    while stack:
        i = stack.pop()
        seq.append(i)
        for j in suc[i]:
            cnt[j] -= 1
            if cnt[j] == 0:
                stack.append(j)
    level = [0.0] * len(ops)
    for i in reversed(seq):
        cost = min([a[1] for a in ops[i]["alts"].values()], default=0.0)
        level[i] = cost + P["sem"] + max([level[j] + (ops[i]["lat"] if ops[j]["deps"].get(i, True) else 0.0) for j in suc[i]], default=ops[i]["lat"])
    x = 12345 + 7919 * P["seed"]
    prio = []
    for i in range(len(ops)):
        x = (x * 1103515245 + 12345) % 2147483648
        prio.append(level[i] - ops[i]["low"] + P["jit"] * x / 2147483648.0)
    ready_at = [0.0] * len(ops)
    free = {e: 0.0 for e in ("vec", "act", "pe", "pool", "sync")}
    order = {e: [] for e in free}
    ready = [i for i, n in enumerate(left) if n == 0]
    while ready:
        pick = None
        for i in ready:
            if not ops[i]["alts"]:
                pick = i
                break
        if pick is None:
            def offers(i):
                qs = list(ops[i]["alts"])
                if len(qs) == 2 and free["act"] <= max(ready_at[i], free["vec"]) + P["vpen"]:
                    return ["act"]
                return qs
            t0, _, _, e = min((max(ready_at[i], free[q]), -prio[i], i, q) for i in ready for q in offers(i))
            cand = [i for i in ready if e in offers(i) and ready_at[i] <= t0 + P["slack"]]
            pick = max(cand, key=lambda i: (prio[i], -i))
            free[e] = max(ready_at[pick], free[e]) + ops[pick]["alts"][e][1]
            order[e].append(pick)
            ops[pick]["eng"] = e
            done = free[e]
        else:
            done = ready_at[pick]
        ready.remove(pick)
        for j in suc[pick]:
            data = ops[j]["deps"].get(pick, True)
            own = not data and list(ops[j]["alts"]) == [ops[pick]["eng"]]
            ready_at[j] = max(ready_at[j], done + (0.0 if own else ops[pick]["lat"] + P["sem"]))
            left[j] -= 1
            if left[j] == 0:
                ready.append(j)
    return order, groups


def emit(g, T, ops, order, groups, sent):
    queue = {"vec": g.vector, "act": g.scalar, "pe": g.tensor, "pool": g, "sync": g.sync}

    def waits_of(o):
        return [j for j, w in o["deps"].items() if w or ops[j]["eng"] != o["eng"]]
    needed = set()
    for o in ops:
        if o["alts"]:
            needed.update(waits_of(o))
    mark = {}
    total = {}
    for e, lst in order.items():
        for i in lst:
            o = ops[i]
            if o["val"]:
                mark[i] = (o["sem"], 16 * len(groups[o["sem"]]))
                total[o["sem"]] = mark[i][1]
            elif o["sem"] is None and i in needed:
                total[ENG_SEM[e]] = total.get(ENG_SEM[e], 0) + 1
                mark[i] = (ENG_SEM[e], total[ENG_SEM[e]])
    for o in ops:
        if not o["alts"]:
            mark[o["i"]] = (o["sem"], o["val"])
    waited = {}
    for e, lst in order.items():
        q, seen = queue[e], {}
        for i in lst:
            o = ops[i]
            want = {}
            for j in waits_of(o):
                s, v = mark[j]
                want[s] = max(want.get(s, 0), v)
            for s, v in want.items():
                if seen.get(s, 0) < v:
                    q.wait_ge(T.sem[s], v)
                    seen[s] = v
                    waited[s] = max(waited.get(s, 0), v)
            r = o["alts"][e][0]()
            if i in mark:
                r.then_inc(T.sem[mark[i][0]], 16 if o["val"] else 1)
    for s, v in total.items():
        if waited.get(s, 0) < v:
            g.sync.wait_ge(T.sem[s], v)
    g.wait_ge(T.sem.sent, sent)


def helper_program(g, core, T, topo, rank, role):
    me, nx, pv = T.cores[rank], T.cores[(rank + 1) % N], T.cores[(rank - 1) % N]
    full = len(topo.engines(me, core))
    part = len(relay_engines(topo, me, core, role))
    jobs = []
    if role == 0:
        jobs.append(("a_rl", full, pv, T.rlx[:]))
        jobs += [("a_b%d" % n, part, nx, T.dl[:, QL * n:QL * n + QL] if PAR["split"] and n < NQ else T.bl[:, 256 + QL * n:256 + QL * n + QL])
                 for n in range(16)]
    elif role == 1:
        jobs += [("a_o%d" % n, part, nx, T.hi[:, QL * n:QL * n + QL] if PAR["split"] and n < NQ else T.ot[:, 256 + QL * n:256 + QL * n + QL])
                 for n in range(16)]
    else:
        jobs += [("a_e%d" % t, full, nx, T.ein[:, 128 * t:128 * t + 128]) for t in range(STEPS - 1)]
    sent = 0
    for sem, n, dst, ap in jobs:
        rid, pid = topo.addr(dst, core)
        g.wait_ge(T.sem[sem], n)
        g.remote_dma(T.rln[:] if sem == "a_rl" else ap, ap, T.sem[sem], T.sem.sent, pid, rid, topo.mask(core, dst))
        sent += len(topo.engines(core, dst))
    g.wait_ge(T.sem.sent, sent)


def rank_program(g, core, T, topo):
    rank = T.rank_of(core)
    if rank is None:
        for r in range(N):
            hs = helpers_of(T, topo, r)[:3]
            if core in hs:
                helper_program(g, core, T, topo, r, hs.index(core))
        return
    ops, sent = build_ops(g, T, topo, rank)
    order, groups = schedule(ops)
    emit(g, T, ops, order, groups, sent)
